import numpy as np
import ml_dtypes


def mxq(x, axis, fmt="e4m3"):
    dtype, down = {"e4m3": (ml_dtypes.float8_e4m3fn, 7), "e5m2": (ml_dtypes.float8_e5m2, 14)}[fmt]
    v = np.moveaxis(np.asarray(x, np.float32).astype(ml_dtypes.bfloat16).astype(np.float64), axis, -1)
    blocks = v.reshape(v.shape[:-1] + (-1, 32))
    amax = np.abs(blocks).max(-1, keepdims=True)
    byte = np.maximum(np.where(amax > 0, np.frexp(amax)[1] - 1 + 127, 0) - down, 1)
    scale = np.exp2(byte - 127.0)
    codes = (blocks / scale).astype(np.float32).astype(dtype).astype(np.float64)
    return np.moveaxis((codes * scale).reshape(v.shape), -1, axis)


WIDE = False


def mx_kscale(k):
    if not WIDE:
        return np.ones(k)
    levels = np.array([10, -10, 5, -5, 0])
    if k % 512:
        return np.exp2(np.random.permutation(np.resize(levels, k // 32))).repeat(32)
    a = np.empty((k // 512, 16))
    for p in range(k // 512):
        a[p, :8] = np.random.permutation(np.resize(levels, 8))
        for g in range(8):
            far = levels[np.abs(levels - a[p, g]) >= 10]
            a[p, g + 8] = far[np.random.randint(len(far))]
    return np.exp2(a.ravel()).repeat(32)


def f64(x):
    return np.asarray(x).astype(np.float64)


def striped(idx):
    return np.tile(np.asarray(idx).reshape(-1, 16).T, (8, 1)).astype(np.uint16)


def unstriped(offs):
    return offs[:16].T.reshape(-1).astype(np.int64)


E2M1 = np.array([0.0, 0.5, 1.0, 1.5, 2.0, 3.0, 4.0, 6.0, -0.0, -0.5, -1.0, -1.5, -2.0, -3.0, -4.0, -6.0])


def pack_weight(w, fmt):
    k, n = w.shape
    w = f64(np.asarray(w, np.float32).astype(ml_dtypes.bfloat16)).reshape(k // 32, 32, n)
    amax = np.abs(w).max(1)
    if fmt == "e4m3":
        byte = np.frexp(amax)[1] - 1 + 127 - 7
    else:
        mant, ex = np.frexp(amax / 6.0)
        byte = np.where(mant > 0.5, ex, ex - 1) + 127
    byte = np.clip(np.where(amax > 0, byte, 1), 1, 254)
    scaled = (w * np.exp2(127.0 - byte)[:, None, :]).reshape(k, n).astype(np.float32)
    by_word = np.ascontiguousarray(scaled.reshape(k // 512, 128, 4, n).transpose(0, 1, 3, 2))
    if fmt == "e4m3":
        words = by_word.astype(ml_dtypes.float8_e4m3fn).view(np.uint8)
    else:
        c = by_word.astype(ml_dtypes.float4_e2m1fn).view(np.uint8) & 0xF
        words = (c[..., 0::2] | (c[..., 1::2] << 4)).reshape(k // 512, 128, 2 * n)
    return np.ascontiguousarray(words), np.ascontiguousarray(byte.astype(np.uint8).reshape(k // 512, 16, n))


def unpack_weight(words, scales, fmt):
    g, _, n = scales.shape
    words = np.ascontiguousarray(words).reshape(g, 128, n, -1)
    if fmt == "e4m3":
        vals = words.view(ml_dtypes.float8_e4m3fn).astype(np.float64)
    else:
        nib = np.empty((g, 128, n, 4), np.uint8)
        nib[..., 0::2] = words & 0xF
        nib[..., 1::2] = words >> 4
        vals = E2M1[nib]
    vals = vals * np.repeat(np.exp2(scales.astype(np.float64) - 127.0), 8, axis=1)[..., None]
    return vals.transpose(0, 1, 3, 2).reshape(g * 512, n)


K, T, J, B, L, N = 512, 2048, 1024, 128, 512, 512


def setup_inputs():
    n = np.random.standard_normal
    idx = (np.random.permutation(T // 8)[:J // 8, None] * 8 + np.arange(8)).reshape(-1)
    fk = mx_kscale(K)
    fl = mx_kscale(L)
    wcp = pack_weight(n((K, N)) * 1 / np.sqrt(K) * fk[:, None], "e4m3")
    xtp = pack_weight(n((L, T)) / fl[:, None], "e4m3")
    wap = pack_weight(n((L, N)) * 1 / np.sqrt(L) * fl[:, None], "e2m1")
    return {
        "xf": (n((K, T)) / fk[:, None]).astype(np.float32),
        "wc_words": wcp[0],
        "wc_scales": wcp[1],
        "xt_words": xtp[0],
        "xt_scales": xtp[1],
        "wa_words": wap[0],
        "wa_scales": wap[1],
        "ga": (np.random.uniform(0.4, 1.2, (1, J))).astype(np.float32),
        "offs": striped(idx),
    }


def reference(xf, wc_words, wc_scales, xt_words, xt_scales, wa_words, wa_scales, ga, offs):
    idx = unstriped(offs)
    wcu = unpack_weight(wc_words, wc_scales, "e4m3")
    xtu = unpack_weight(xt_words, xt_scales, "e4m3")
    wau = unpack_weight(wa_words, wa_scales, "e2m1")
    m1 = f64(xf)[:, idx].reshape(K, B, J // B).mean(axis=2)
    m2 = 2.0 * m1
    m2q = mxq(m2, 0, "e4m3")
    q = wcu.T @ m2q
    qr = np.repeat(q, J // B, axis=1)
    xtidxg = xtu[:, idx]
    p = wau.T @ xtidxg
    y = np.maximum(p + qr, 0.0) * f64(ga)
    return y

@@ -1,0 +1,151 @@
+from contextlib import ExitStack
+
+import concourse.mybir as mybir
+from concourse.masks import make_identity
+
+K, T, J, B, L, N = 512, 2048, 1024, 128, 512, 512
+FLOPS = 2 * K * N * B + 2 * L * N * J
+
+F32 = mybir.dt.float32
+BF16 = mybir.dt.bfloat16
+I32 = mybir.dt.int32
+U32 = mybir.dt.uint32
+U16 = mybir.dt.uint16
+U8 = mybir.dt.uint8
+FP8X4 = mybir.dt.float8_e4m3fn_x4
+FP4X4 = mybir.dt.float4_e2m1fn_x4
+ALU = mybir.AluOpType
+ACT = mybir.ActivationFunctionType
+
+P = 128
+PACK = 4
+RUN = 8
+BANK = 512
+HALVES = J // BANK
+HALF_BLOCKS = B // HALVES
+LIST_COL = 16
+PAIR = 2
+
+
+def load_scale_rows(nc, plane, scales):
+    for r in range(4):
+        nc.sync.dma_start(out=plane[r:P:32, :].bitcast(I32), in_=scales[0, r:16:4, :].bitcast(I32))
+
+
+def tile_moe_expert_with_block_context_kernel(tc, xf, wc_words, wc_scales, xt_words, xt_scales, wa_words, wa_scales, ga, offs, out):
+    nc = tc.nc
+    with ExitStack() as ctx:
+        keep = ctx.enter_context(tc.tile_pool(name="keep", bufs=1))
+        psum = ctx.enter_context(tc.psum_pool(name="psum", bufs=1))
+
+        def bank(i):
+            return psum.tile([P, BANK], F32, name=f"bank{i}", tag=f"bank{i}")
+
+        offsets = keep.tile([P, J // LIST_COL], U16, name="offsets")
+        xt_plane = keep.tile([P, T], U8, name="xt_plane", align_bytes=64)
+        wa_plane = keep.tile([P, N], U8, name="wa_plane", align_bytes=64)
+        wc_plane = keep.tile([P, N], U8, name="wc_plane", align_bytes=64)
+        xt_codes = keep.tile([P, T], I32, name="xt_codes", align_bytes=64)
+        wa_codes = keep.tile([P, 2 * N], U8, name="wa_codes", align_bytes=64)
+        wc_codes = keep.tile([P, N], I32, name="wc_codes", align_bytes=64)
+        xf_rows = [keep.tile([P, T], F32, name=f"xf_rows{t}", align_bytes=64) for t in range(PACK)]
+        ga_runs = keep.tile([P, RUN], F32, name="ga_runs")
+        ident = keep.tile([P, P], F32, name="ident", align_bytes=64)
+
+        nc.vector.memset(xt_plane[:].bitcast(I32), 0)
+        nc.vector.memset(wa_plane[:].bitcast(I32), 0)
+        nc.vector.memset(wc_plane[:].bitcast(I32), 0)
+        make_identity(nc, ident[:])
+
+        xf_by_slot = xf.rearrange("(p t) c -> t p c", t=PACK)
+        nc.sync.dma_start(offsets[:], offs)
+        nc.sync.dma_start(out=xt_codes[:], in_=xt_words[0].rearrange("p c r -> p (c r)").bitcast(I32))
+        load_scale_rows(nc, xt_plane, xt_scales)
+        nc.sync.dma_start(out=xf_rows[0][:], in_=xf_by_slot[0])
+        nc.sync.dma_start(out=ga_runs[:], in_=ga.rearrange("o (b r) -> (o b) r", r=RUN))
+        nc.sync.dma_start(out=wa_codes[:].bitcast(I32), in_=wa_words[0].bitcast(I32))
+        load_scale_rows(nc, wa_plane, wa_scales)
+        for t in range(1, PACK):
+            nc.sync.dma_start(out=xf_rows[t][:], in_=xf_by_slot[t])
+        nc.sync.dma_start(out=wc_codes[:], in_=wc_words[0].rearrange("p c r -> p (c r)").bitcast(I32))
+        load_scale_rows(nc, wc_plane, wc_scales)
+
+        def half_list(h):
+            cols = BANK // LIST_COL
+            return offsets[:, h * cols:(h + 1) * cols]
+
+        ga_all = keep.tile([P, B, RUN], F32, name="ga_all")
+        for a in range(2):
+            spread = bank(6 + a)
+            for r in range(4):
+                col = 4 * a + r
+                nc.tensor.transpose(spread[:, r * P:(r + 1) * P], ga_runs[:, col:col + 1].to_broadcast([P, P]), ident[:])
+            nc.scalar.copy(ga_all[:, :, 4 * a:4 * a + 4], spread[:].rearrange("p (r b) -> p b r", r=4))
+
+        tok_plane = keep.tile([P, J], U8, name="tok_plane", align_bytes=64)
+        nc.vector.tensor_copy(tok_plane[:], xt_plane[:].indirect(offsets[:]))
+        tok_codes = []
+        for h in range(HALVES):
+            codes = keep.tile([P, BANK], U32, name=f"tok_codes{h}", align_bytes=64)
+            nc.vector.tensor_copy(codes[:], xt_codes[:].bitcast(U32).indirect(half_list(h)))
+            tok_codes.append(codes)
+
+        p_t = []
+        for s in range(J // P):
+            h, i = divmod(s, BANK // P)
+            acc = bank(4 + i)
+            nc.tensor.matmul_mx(out=acc[:], lhsT=tok_codes[h][:, i * P:(i + 1) * P].bitcast(FP8X4),
+                                lhsT_scale=tok_plane[:, s * P:(s + 1) * P],
+                                rhs=wa_codes[:].bitcast(FP4X4), rhs_scale=wa_plane[:], start=True, stop=True)
+            sb = keep.tile([P, N], F32, name=f"p_t{s}", align_bytes=64)
+            nc.scalar.copy(sb[:], acc[:])
+            p_t.append(sb)
+
+        def open_sum(h, m):
+            acc = bank(4 * h + m)
+            for i in range(BANK // P):
+                nc.tensor.matmul(acc[:, i * P:(i + 1) * P], lhsT=p_t[4 * h + i][:, m * P:(m + 1) * P], rhs=ident[:],
+                                 is_transpose=True, start=(i == 0), stop=False)
+            return acc
+
+        tiles = [(h, m) for h in range(HALVES) for m in range(N // P)]
+        sums_open = {hm: open_sum(*hm) for hm in tiles[:-1]}
+
+        sums = keep.tile([P, PACK, B], F32, name="sums")
+        for t in range(PACK - 1):
+            picked = keep.tile([P, J], F32, name=f"picked{t}")
+            nc.vector.tensor_copy(picked[:], xf_rows[t][:].indirect(offsets[:]))
+            nc.vector.tensor_reduce(sums[:, t, :], picked[:].rearrange("p (b r) -> p b r", r=RUN), mybir.AxisListType.X, ALU.add)
+        last = PACK - 1
+        picked_last = []
+        for h in range(HALVES):
+            picked = keep.tile([P, BANK], F32, name=f"picked_last{h}")
+            nc.vector.tensor_copy(picked[:], xf_rows[last][:].indirect(half_list(h)))
+            picked_last.append(picked)
+        q_t = []
+        for h in range(HALVES):
+            blocks = slice(h * HALF_BLOCKS, (h + 1) * HALF_BLOCKS)
+            nc.vector.tensor_reduce(sums[:, last, blocks], picked_last[h][:].rearrange("p (b r) -> p b r", r=RUN), mybir.AxisListType.X, ALU.add)
+            m2 = keep.tile([P, HALF_BLOCKS, PAIR, PACK], BF16, name=f"m2_{h}", align_bytes=64)
+            twice = sums[:, :, blocks].rearrange("p t b -> p b t").unsqueeze(2).to_broadcast([P, HALF_BLOCKS, PAIR, PACK])
+            nc.scalar.activation(m2[:], twice, ACT.Copy, scale=2.0 / RUN)
+            m2_codes = keep.tile([P, P], U32, name=f"m2_codes{h}", align_bytes=64)
+            m2_plane = keep.tile([P, P], U8, name=f"m2_plane{h}", align_bytes=64)
+            nc.vector.quantize_mx(out=m2_codes[:].bitcast(FP8X4), scales=m2_plane[:], in_=m2[:].rearrange("p b d t -> p (b d t)"))
+            acc = bank(7)
+            nc.tensor.matmul_mx(out=acc[:], lhsT=m2_codes[:].bitcast(FP8X4), lhsT_scale=m2_plane[:],
+                                rhs=wc_codes[:].bitcast(FP8X4), rhs_scale=wc_plane[:], start=True, stop=True)
+            sb = keep.tile([P, N], F32, name=f"q_t{h}", align_bytes=64)
+            nc.scalar.copy(sb[:], acc[:])
+            q_t.append(sb)
+
+        for h, m in tiles:
+            acc = sums_open[(h, m)] if (h, m) in sums_open else open_sum(h, m)
+            pairs = acc[:].rearrange("p (b u e) -> p b u e", u=RUN // PAIR, e=PAIR)
+            for u in range(RUN // PAIR):
+                nc.tensor.matmul(pairs[:, :, u, :], lhsT=q_t[h][:, m * P:(m + 1) * P], rhs=ident[:],
+                                 is_transpose=True, start=False, stop=(u == RUN // PAIR - 1))
+            res = keep.tile([P, BANK], F32, name=f"res{h}_{m}")
+            gate = ga_all[:, h * HALF_BLOCKS:(h + 1) * HALF_BLOCKS, :].rearrange("p b r -> p (b r)")
+            nc.vector.scalar_tensor_tensor(res[:], acc[:], 0.0, gate, ALU.max, ALU.mult)
+            nc.sync.dma_start(out=out[m * P:(m + 1) * P, h * BANK:(h + 1) * BANK], in_=res[:])

@@ -24,7 +24,9 @@ BANK = 512
 HALVES = J // BANK
 HALF_BLOCKS = B // HALVES
 LIST_COL = 16
-PAIR = 2
+WORK_BANKS = 6
+PE_PLANES = 3
+POOL_TILES = (0, 1, 3, 5)
 
 
 def load_scale_rows(nc, plane, scales):
@@ -39,7 +41,7 @@ def tile_moe_expert_with_block_context_kernel(tc, xf, wc_words, wc_scales, xt_wo
         psum = ctx.enter_context(tc.psum_pool(name="psum", bufs=1))
 
         def bank(i):
-            return psum.tile([P, BANK], F32, name=f"bank{i}", tag=f"bank{i}")
+            return psum.tile([P, BANK], F32, name=f"work{i % WORK_BANKS}", tag=f"work{i % WORK_BANKS}")
 
         offsets = keep.tile([P, J // LIST_COL], U16, name="offsets")
         xt_plane = keep.tile([P, T], U8, name="xt_plane", align_bytes=64)
@@ -49,103 +51,111 @@ def tile_moe_expert_with_block_context_kernel(tc, xf, wc_words, wc_scales, xt_wo
         wa_codes = keep.tile([P, 2 * N], U8, name="wa_codes", align_bytes=64)
         wc_codes = keep.tile([P, N], I32, name="wc_codes", align_bytes=64)
         xf_rows = [keep.tile([P, T], F32, name=f"xf_rows{t}", align_bytes=64) for t in range(PACK)]
-        ga_runs = keep.tile([P, RUN], F32, name="ga_runs")
+        ga_rows = keep.tile([P, P], F32, name="ga_rows", align_bytes=64)
         ident = keep.tile([P, P], F32, name="ident", align_bytes=64)
 
         nc.vector.memset(xt_plane[:].bitcast(I32), 0)
+        nc.vector.memset(ga_rows[:], 0.0)
         nc.vector.memset(wa_plane[:].bitcast(I32), 0)
         nc.vector.memset(wc_plane[:].bitcast(I32), 0)
         make_identity(nc, ident[:])
 
         xf_by_slot = xf.rearrange("(p t) c -> t p c", t=PACK)
         nc.sync.dma_start(offsets[:], offs)
-        nc.sync.dma_start(out=xt_codes[:], in_=xt_words[0].rearrange("p c r -> p (c r)").bitcast(I32))
-        load_scale_rows(nc, xt_plane, xt_scales)
         nc.sync.dma_start(out=xf_rows[0][:], in_=xf_by_slot[0])
-        nc.sync.dma_start(out=ga_runs[:], in_=ga.rearrange("o (b r) -> (o b) r", r=RUN))
-        nc.sync.dma_start(out=wa_codes[:].bitcast(I32), in_=wa_words[0].bitcast(I32))
-        load_scale_rows(nc, wa_plane, wa_scales)
-        for t in range(1, PACK):
-            nc.sync.dma_start(out=xf_rows[t][:], in_=xf_by_slot[t])
-        nc.sync.dma_start(out=wc_codes[:], in_=wc_words[0].rearrange("p c r -> p (c r)").bitcast(I32))
+        load_scale_rows(nc, xt_plane, xt_scales)
+        nc.sync.dma_start(out=ga_rows[0:J // P, :], in_=ga.rearrange("o (s i) -> (o s) i", i=P))
+        nc.sync.dma_start(out=xf_rows[1][:], in_=xf_by_slot[1])
         load_scale_rows(nc, wc_plane, wc_scales)
+        nc.sync.dma_start(out=xf_rows[2][:], in_=xf_by_slot[2])
+        load_scale_rows(nc, wa_plane, wa_scales)
+        nc.sync.dma_start(out=xf_rows[3][:], in_=xf_by_slot[3])
+        nc.sync.dma_start(out=xt_codes[:], in_=xt_words[0].rearrange("p c r -> p (c r)").bitcast(I32))
+        nc.sync.dma_start(out=wc_codes[:], in_=wc_words[0].rearrange("p c r -> p (c r)").bitcast(I32))
+        nc.sync.dma_start(out=wa_codes[:].bitcast(I32), in_=wa_words[0].bitcast(I32))
 
         def half_list(h):
             cols = BANK // LIST_COL
             return offsets[:, h * cols:(h + 1) * cols]
 
-        ga_all = keep.tile([P, B, RUN], F32, name="ga_all")
-        for a in range(2):
-            spread = bank(6 + a)
-            for r in range(4):
-                col = 4 * a + r
-                nc.tensor.transpose(spread[:, r * P:(r + 1) * P], ga_runs[:, col:col + 1].to_broadcast([P, P]), ident[:])
-            nc.scalar.copy(ga_all[:, :, 4 * a:4 * a + 4], spread[:].rearrange("p (r b) -> p b r", r=4))
+        turned = bank(0)
+        nc.tensor.transpose(turned[:, 0:P], ga_rows[:], ident[:])
+        ga_cols = keep.tile([P, J // P], F32, name="ga_cols")
+        nc.scalar.copy(ga_cols[:], turned[:, 0:J // P])
+        gate_psum = [psum.tile([P, BANK], F32, name=f"gate{h}", tag=f"gate{h}") for h in range(HALVES)]
+        for s in range(J // P):
+            h, i = divmod(s, BANK // P)
+            nc.tensor.transpose(gate_psum[h][:, i * P:(i + 1) * P], ga_cols[:, s:s + 1].to_broadcast([P, P]), ident[:])
+        gate_sbuf = keep.tile([P, J], F32, name="gate_sbuf")
+        for h in range(HALVES):
+            nc.scalar.copy(gate_sbuf[:, h * BANK:(h + 1) * BANK], gate_psum[h][:])
 
         tok_plane = keep.tile([P, J], U8, name="tok_plane", align_bytes=64)
         nc.vector.tensor_copy(tok_plane[:], xt_plane[:].indirect(offsets[:]))
-        tok_codes = []
-        for h in range(HALVES):
-            codes = keep.tile([P, BANK], U32, name=f"tok_codes{h}", align_bytes=64)
-            nc.vector.tensor_copy(codes[:], xt_codes[:].bitcast(U32).indirect(half_list(h)))
-            tok_codes.append(codes)
-
-        p_t = []
-        for s in range(J // P):
-            h, i = divmod(s, BANK // P)
-            acc = bank(4 + i)
-            nc.tensor.matmul_mx(out=acc[:], lhsT=tok_codes[h][:, i * P:(i + 1) * P].bitcast(FP8X4),
-                                lhsT_scale=tok_plane[:, s * P:(s + 1) * P],
-                                rhs=wa_codes[:].bitcast(FP4X4), rhs_scale=wa_plane[:], start=True, stop=True)
-            sb = keep.tile([P, N], F32, name=f"p_t{s}", align_bytes=64)
-            nc.scalar.copy(sb[:], acc[:])
-            p_t.append(sb)
-
-        def open_sum(h, m):
-            acc = bank(4 * h + m)
-            for i in range(BANK // P):
-                nc.tensor.matmul(acc[:, i * P:(i + 1) * P], lhsT=p_t[4 * h + i][:, m * P:(m + 1) * P], rhs=ident[:],
-                                 is_transpose=True, start=(i == 0), stop=False)
-            return acc
-
-        tiles = [(h, m) for h in range(HALVES) for m in range(N // P)]
-        sums_open = {hm: open_sum(*hm) for hm in tiles[:-1]}
 
         sums = keep.tile([P, PACK, B], F32, name="sums")
-        for t in range(PACK - 1):
-            picked = keep.tile([P, J], F32, name=f"picked{t}")
+        for t in range(PACK):
+            picked = keep.tile([P, J], F32, name=f"picked{t}", align_bytes=64)
             nc.vector.tensor_copy(picked[:], xf_rows[t][:].indirect(offsets[:]))
-            nc.vector.tensor_reduce(sums[:, t, :], picked[:].rearrange("p (b r) -> p b r", r=RUN), mybir.AxisListType.X, ALU.add)
-        last = PACK - 1
-        picked_last = []
-        for h in range(HALVES):
-            picked = keep.tile([P, BANK], F32, name=f"picked_last{h}")
-            nc.vector.tensor_copy(picked[:], xf_rows[last][:].indirect(half_list(h)))
-            picked_last.append(picked)
-        q_t = []
-        for h in range(HALVES):
-            blocks = slice(h * HALF_BLOCKS, (h + 1) * HALF_BLOCKS)
-            nc.vector.tensor_reduce(sums[:, last, blocks], picked_last[h][:].rearrange("p (b r) -> p b r", r=RUN), mybir.AxisListType.X, ALU.add)
-            m2 = keep.tile([P, HALF_BLOCKS, PAIR, PACK], BF16, name=f"m2_{h}", align_bytes=64)
-            twice = sums[:, :, blocks].rearrange("p t b -> p b t").unsqueeze(2).to_broadcast([P, HALF_BLOCKS, PAIR, PACK])
-            nc.scalar.activation(m2[:], twice, ACT.Copy, scale=2.0 / RUN)
-            m2_codes = keep.tile([P, P], U32, name=f"m2_codes{h}", align_bytes=64)
-            m2_plane = keep.tile([P, P], U8, name=f"m2_plane{h}", align_bytes=64)
-            nc.vector.quantize_mx(out=m2_codes[:].bitcast(FP8X4), scales=m2_plane[:], in_=m2[:].rearrange("p b d t -> p (b d t)"))
-            acc = bank(7)
-            nc.tensor.matmul_mx(out=acc[:], lhsT=m2_codes[:].bitcast(FP8X4), lhsT_scale=m2_plane[:],
-                                rhs=wc_codes[:].bitcast(FP8X4), rhs_scale=wc_plane[:], start=True, stop=True)
-            sb = keep.tile([P, N], F32, name=f"q_t{h}", align_bytes=64)
-            nc.scalar.copy(sb[:], acc[:])
-            q_t.append(sb)
+            runs = picked[:].rearrange("p (b r) -> p b r", r=RUN)
+            if t < PE_PLANES:
+                acc = bank(1 + t % 2)
+                for r in range(RUN):
+                    nc.tensor.matmul(acc[:, 0:P], lhsT=runs[:, :, r], rhs=ident[:], is_transpose=True, start=(r == 0), stop=(r == RUN - 1))
+                sums_t = keep.tile([P, P], F32, name=f"sums_t{t}", align_bytes=64)
+                nc.scalar.copy(sums_t[:], acc[:, 0:P])
+                back = bank(3 + t % 2)
+                nc.tensor.transpose(back[:, 0:P], sums_t[:], ident[:])
+                nc.scalar.copy(sums[:, t, :], back[:, 0:P])
+            else:
+                nc.vector.tensor_reduce(sums[:, t, :], runs, mybir.AxisListType.X, ALU.add)
 
-        for h, m in tiles:
-            acc = sums_open[(h, m)] if (h, m) in sums_open else open_sum(h, m)
-            pairs = acc[:].rearrange("p (b u e) -> p b u e", u=RUN // PAIR, e=PAIR)
-            for u in range(RUN // PAIR):
-                nc.tensor.matmul(pairs[:, :, u, :], lhsT=q_t[h][:, m * P:(m + 1) * P], rhs=ident[:],
-                                 is_transpose=True, start=False, stop=(u == RUN // PAIR - 1))
-            res = keep.tile([P, BANK], F32, name=f"res{h}_{m}")
-            gate = ga_all[:, h * HALF_BLOCKS:(h + 1) * HALF_BLOCKS, :].rearrange("p b r -> p (b r)")
-            nc.vector.scalar_tensor_tensor(res[:], acc[:], 0.0, gate, ALU.max, ALU.mult)
+        m2 = keep.tile([P, B, PACK], BF16, name="m2", tag="staging", align_bytes=64)
+        nc.scalar.activation(m2[:], sums[:].rearrange("p t b -> p b t"), ACT.Copy, scale=2.0 / RUN)
+
+        tok_codes = [keep.tile([P, BANK], U32, name="tok_codes0", align_bytes=64)]
+        nc.vector.tensor_copy(tok_codes[0][:], xt_codes[:].bitcast(U32).indirect(half_list(0)))
+        m2_codes = keep.tile([P, B], U32, name="m2_codes", align_bytes=64)
+        m2_plane = keep.tile([P, B], U8, name="m2_plane", align_bytes=64)
+        nc.vector.quantize_mx(out=m2_codes[:].bitcast(FP8X4), scales=m2_plane[:], in_=m2[:].rearrange("p b t -> p (b t)"))
+        tok_codes.append(keep.tile([P, BANK], U32, name="tok_codes1", tag="staging", align_bytes=64))
+        nc.vector.tensor_copy(tok_codes[1][:], xt_codes[:].bitcast(U32).indirect(half_list(1)))
+
+        q_acc = bank(5)
+        for m in range(N // P):
+            cols = slice(m * P, (m + 1) * P)
+            nc.tensor.matmul_mx(out=q_acc[:, cols], lhsT=wc_codes[:, cols].bitcast(FP8X4), lhsT_scale=wc_plane[:, cols],
+                                rhs=m2_codes[:].bitcast(FP8X4), rhs_scale=m2_plane[:], start=True, stop=True)
+        q = keep.tile([P, N // P, B], F32, name="q")
+        nc.scalar.copy(q[:], q_acc[:].rearrange("p (m b) -> p m b", b=B))
+
+        tiles = [(h, m) for h in range(HALVES) for m in range(N // P)]
+
+        def add_context(i):
+            h, m = tiles[i]
+            acc = bank(i)
+            nc.tensor.matmul_mx(out=acc[:], lhsT=wa_codes[:, 2 * m * P:2 * (m + 1) * P].bitcast(FP4X4), lhsT_scale=wa_plane[:, m * P:(m + 1) * P],
+                                rhs=tok_codes[h][:].bitcast(FP8X4), rhs_scale=tok_plane[:, h * BANK:(h + 1) * BANK], start=True, stop=True)
+            summed = keep.tile([P, BANK], F32, name=f"summed{i}")
+            q_run = q[:, m, h * HALF_BLOCKS:(h + 1) * HALF_BLOCKS].unsqueeze(2).to_broadcast([P, HALF_BLOCKS, RUN])
+            nc.vector.tensor_tensor(summed[:].rearrange("p (b r) -> p b r", r=RUN), acc[:].rearrange("p (b r) -> p b r", r=RUN), q_run, ALU.add)
+            return summed
+
+        def finish(i, summed):
+            h, m = tiles[i]
+            res = keep.tile([P, BANK], F32, name=f"res{i}")
+            if i in POOL_TILES:
+                cut = keep.tile([P, BANK], F32, name=f"cut{i}")
+                nc.scalar.activation(cut[:], summed[:], ACT.Relu)
+                nc.gpsimd.tensor_tensor(res[:], cut[:], gate_sbuf[:, h * BANK:(h + 1) * BANK], ALU.mult)
+            else:
+                nc.vector.scalar_tensor_tensor(res[:], summed[:], 0.0, gate_psum[h][:], ALU.max, ALU.mult)
             nc.sync.dma_start(out=out[m * P:(m + 1) * P, h * BANK:(h + 1) * BANK], in_=res[:])
+
+        behind = None
+        for i in range(len(tiles)):
+            summed = add_context(i)
+            if behind is not None:
+                finish(i - 1, behind)
+            behind = summed
+        finish(len(tiles) - 1, behind)

@@ -25,7 +25,8 @@ HALVES = J // BANK
 HALF_BLOCKS = B // HALVES
 LIST_COL = 16
 WORK_BANKS = 6
-PE_PLANES = 3
+HEAD = 512
+PE_PLANES = 2
 POOL_TILES = (0, 1, 3, 5)
 
 
@@ -62,8 +63,9 @@ def tile_moe_expert_with_block_context_kernel(tc, xf, wc_words, wc_scales, xt_wo
 
         xf_by_slot = xf.rearrange("(p t) c -> t p c", t=PACK)
         nc.sync.dma_start(offsets[:], offs)
-        nc.sync.dma_start(out=xf_rows[0][:], in_=xf_by_slot[0])
+        nc.sync.dma_start(out=xf_rows[0][:, 0:HEAD], in_=xf_by_slot[0][:, 0:HEAD])
         load_scale_rows(nc, xt_plane, xt_scales)
+        nc.sync.dma_start(out=xf_rows[0][:, HEAD:T], in_=xf_by_slot[0][:, HEAD:T])
         nc.sync.dma_start(out=ga_rows[0:J // P, :], in_=ga.rearrange("o (s i) -> (o s) i", i=P))
         nc.sync.dma_start(out=xf_rows[1][:], in_=xf_by_slot[1])
         load_scale_rows(nc, wc_plane, wc_scales)

@@ -24,10 +24,9 @@ BANK = 512
 HALVES = J // BANK
 HALF_BLOCKS = B // HALVES
 LIST_COL = 16
-WORK_BANKS = 6
+PAIR = 2
 HEAD = 512
-PE_PLANES = 2
-POOL_TILES = (0, 1, 3, 5)
+PE_PLANES = 3
 
 
 def load_scale_rows(nc, plane, scales):
@@ -42,7 +41,7 @@ def tile_moe_expert_with_block_context_kernel(tc, xf, wc_words, wc_scales, xt_wo
         psum = ctx.enter_context(tc.psum_pool(name="psum", bufs=1))
 
         def bank(i):
-            return psum.tile([P, BANK], F32, name=f"work{i % WORK_BANKS}", tag=f"work{i % WORK_BANKS}")
+            return psum.tile([P, BANK], F32, name=f"bank{i}", tag=f"bank{i}")
 
         offsets = keep.tile([P, J // LIST_COL], U16, name="offsets")
         xt_plane = keep.tile([P, T], U8, name="xt_plane", align_bytes=64)
@@ -84,13 +83,13 @@ def tile_moe_expert_with_block_context_kernel(tc, xf, wc_words, wc_scales, xt_wo
         nc.tensor.transpose(turned[:, 0:P], ga_rows[:], ident[:])
         ga_cols = keep.tile([P, J // P], F32, name="ga_cols")
         nc.scalar.copy(ga_cols[:], turned[:, 0:J // P])
-        gate_psum = [psum.tile([P, BANK], F32, name=f"gate{h}", tag=f"gate{h}") for h in range(HALVES)]
-        for s in range(J // P):
-            h, i = divmod(s, BANK // P)
-            nc.tensor.transpose(gate_psum[h][:, i * P:(i + 1) * P], ga_cols[:, s:s + 1].to_broadcast([P, P]), ident[:])
-        gate_sbuf = keep.tile([P, J], F32, name="gate_sbuf")
+        gate = keep.tile([P, J], F32, name="gate")
         for h in range(HALVES):
-            nc.scalar.copy(gate_sbuf[:, h * BANK:(h + 1) * BANK], gate_psum[h][:])
+            spread = bank(6 + h)
+            for i in range(BANK // P):
+                s = h * (BANK // P) + i
+                nc.tensor.transpose(spread[:, i * P:(i + 1) * P], ga_cols[:, s:s + 1].to_broadcast([P, P]), ident[:])
+            nc.scalar.copy(gate[:, h * BANK:(h + 1) * BANK], spread[:])
 
         tok_plane = keep.tile([P, J], U8, name="tok_plane", align_bytes=64)
         nc.vector.tensor_copy(tok_plane[:], xt_plane[:].indirect(offsets[:]))
@@ -112,52 +111,84 @@ def tile_moe_expert_with_block_context_kernel(tc, xf, wc_words, wc_scales, xt_wo
             else:
                 nc.vector.tensor_reduce(sums[:, t, :], runs, mybir.AxisListType.X, ALU.add)
 
-        m2 = keep.tile([P, B, PACK], BF16, name="m2", tag="staging", align_bytes=64)
-        nc.scalar.activation(m2[:], sums[:].rearrange("p t b -> p b t"), ACT.Copy, scale=2.0 / RUN)
+        by_block = sums[:].rearrange("p t b -> p b t")
+        m2_lo = keep.tile([P, HALF_BLOCKS, PACK], BF16, name="m2_lo", align_bytes=64)
+        nc.scalar.activation(m2_lo[:], by_block[:, 0:HALF_BLOCKS, :], ACT.Copy, scale=2.0 / RUN)
+        m2_hi = keep.tile([P, HALF_BLOCKS, PAIR, PACK], BF16, name="m2_hi", tag="staging", align_bytes=64)
+        twice = by_block[:, HALF_BLOCKS:B, :].unsqueeze(2).to_broadcast([P, HALF_BLOCKS, PAIR, PACK])
+        nc.scalar.activation(m2_hi[:], twice, ACT.Copy, scale=2.0 / RUN)
 
-        tok_codes = [keep.tile([P, BANK], U32, name="tok_codes0", align_bytes=64)]
-        nc.vector.tensor_copy(tok_codes[0][:], xt_codes[:].bitcast(U32).indirect(half_list(0)))
-        m2_codes = keep.tile([P, B], U32, name="m2_codes", align_bytes=64)
-        m2_plane = keep.tile([P, B], U8, name="m2_plane", align_bytes=64)
-        nc.vector.quantize_mx(out=m2_codes[:].bitcast(FP8X4), scales=m2_plane[:], in_=m2[:].rearrange("p b t -> p (b t)"))
-        tok_codes.append(keep.tile([P, BANK], U32, name="tok_codes1", tag="staging", align_bytes=64))
-        nc.vector.tensor_copy(tok_codes[1][:], xt_codes[:].bitcast(U32).indirect(half_list(1)))
+        tok_lo = keep.tile([P, BANK], U32, name="tok_lo", align_bytes=64)
+        nc.vector.tensor_copy(tok_lo[:], xt_codes[:].bitcast(U32).indirect(half_list(0)))
+        lo_codes = keep.tile([P, HALF_BLOCKS], U32, name="lo_codes", align_bytes=64)
+        lo_plane = keep.tile([P, HALF_BLOCKS], U8, name="lo_plane", align_bytes=64)
+        nc.vector.quantize_mx(out=lo_codes[:].bitcast(FP8X4), scales=lo_plane[:], in_=m2_lo[:].rearrange("p b t -> p (b t)"))
+        hi_codes = keep.tile([P, P], U32, name="hi_codes", align_bytes=64)
+        hi_plane = keep.tile([P, P], U8, name="hi_plane", align_bytes=64)
+        nc.vector.quantize_mx(out=hi_codes[:].bitcast(FP8X4), scales=hi_plane[:], in_=m2_hi[:].rearrange("p b d t -> p (b d t)"))
+        tok_hi = keep.tile([P, BANK], U32, name="tok_hi", tag="staging", align_bytes=64)
+        nc.vector.tensor_copy(tok_hi[:], xt_codes[:].bitcast(U32).indirect(half_list(1)))
 
-        q_acc = bank(5)
+        q_acc = bank(0)
         for m in range(N // P):
             cols = slice(m * P, (m + 1) * P)
-            nc.tensor.matmul_mx(out=q_acc[:, cols], lhsT=wc_codes[:, cols].bitcast(FP8X4), lhsT_scale=wc_plane[:, cols],
-                                rhs=m2_codes[:].bitcast(FP8X4), rhs_scale=m2_plane[:], start=True, stop=True)
-        q = keep.tile([P, N // P, B], F32, name="q")
-        nc.scalar.copy(q[:], q_acc[:].rearrange("p (m b) -> p m b", b=B))
+            nc.tensor.matmul_mx(out=q_acc[:, m * HALF_BLOCKS:(m + 1) * HALF_BLOCKS], lhsT=wc_codes[:, cols].bitcast(FP8X4), lhsT_scale=wc_plane[:, cols],
+                                rhs=lo_codes[:].bitcast(FP8X4), rhs_scale=lo_plane[:], start=True, stop=True)
+        q_lo = keep.tile([P, N // P, HALF_BLOCKS], F32, name="q_lo")
+        nc.scalar.copy(q_lo[:], q_acc[:, 0:N // P * HALF_BLOCKS].rearrange("p (m b) -> p m b", b=HALF_BLOCKS))
 
-        tiles = [(h, m) for h in range(HALVES) for m in range(N // P)]
-
-        def add_context(i):
-            h, m = tiles[i]
-            acc = bank(i)
-            nc.tensor.matmul_mx(out=acc[:], lhsT=wa_codes[:, 2 * m * P:2 * (m + 1) * P].bitcast(FP4X4), lhsT_scale=wa_plane[:, m * P:(m + 1) * P],
-                                rhs=tok_codes[h][:].bitcast(FP8X4), rhs_scale=tok_plane[:, h * BANK:(h + 1) * BANK], start=True, stop=True)
-            summed = keep.tile([P, BANK], F32, name=f"summed{i}")
-            q_run = q[:, m, h * HALF_BLOCKS:(h + 1) * HALF_BLOCKS].unsqueeze(2).to_broadcast([P, HALF_BLOCKS, RUN])
-            nc.vector.tensor_tensor(summed[:].rearrange("p (b r) -> p b r", r=RUN), acc[:].rearrange("p (b r) -> p b r", r=RUN), q_run, ALU.add)
-            return summed
-
-        def finish(i, summed):
-            h, m = tiles[i]
-            res = keep.tile([P, BANK], F32, name=f"res{i}")
-            if i in POOL_TILES:
-                cut = keep.tile([P, BANK], F32, name=f"cut{i}")
-                nc.scalar.activation(cut[:], summed[:], ACT.Relu)
-                nc.gpsimd.tensor_tensor(res[:], cut[:], gate_sbuf[:, h * BANK:(h + 1) * BANK], ALU.mult)
-            else:
-                nc.vector.scalar_tensor_tensor(res[:], summed[:], 0.0, gate_psum[h][:], ALU.max, ALU.mult)
+        def store(res, h, m):
             nc.sync.dma_start(out=out[m * P:(m + 1) * P, h * BANK:(h + 1) * BANK], in_=res[:])
 
-        behind = None
-        for i in range(len(tiles)):
-            summed = add_context(i)
-            if behind is not None:
-                finish(i - 1, behind)
-            behind = summed
-        finish(len(tiles) - 1, behind)
+        def p_lo(m, b):
+            acc = bank(b)
+            nc.tensor.matmul_mx(out=acc[:], lhsT=wa_codes[:, 2 * m * P:2 * (m + 1) * P].bitcast(FP4X4), lhsT_scale=wa_plane[:, m * P:(m + 1) * P],
+                                rhs=tok_lo[:].bitcast(FP8X4), rhs_scale=tok_plane[:, 0:BANK], start=True, stop=True)
+            return acc
+
+        p_acc = [p_lo(0, 2), p_lo(1, 3)]
+
+        qt_acc = bank(1)
+        nc.tensor.matmul_mx(out=qt_acc[:], lhsT=hi_codes[:].bitcast(FP8X4), lhsT_scale=hi_plane[:],
+                            rhs=wc_codes[:].bitcast(FP8X4), rhs_scale=wc_plane[:], start=True, stop=True)
+        q_t = keep.tile([P, N], F32, name="q_t", align_bytes=64)
+        nc.scalar.copy(q_t[:], qt_acc[:])
+        p_acc.extend([p_lo(2, 0), p_lo(3, 1)])
+
+        p_t = []
+        for i in range(BANK // P):
+            acc = bank(4 + i)
+            nc.tensor.matmul_mx(out=acc[:], lhsT=tok_hi[:, i * P:(i + 1) * P].bitcast(FP8X4),
+                                lhsT_scale=tok_plane[:, BANK + i * P:BANK + (i + 1) * P],
+                                rhs=wa_codes[:].bitcast(FP4X4), rhs_scale=wa_plane[:], start=True, stop=True)
+            sb = keep.tile([P, N], F32, name=f"p_t{i}", align_bytes=64)
+            nc.scalar.copy(sb[:], acc[:])
+            p_t.append(sb)
+
+        def add_context(m):
+            summed = keep.tile([P, BANK], F32, name=f"summed{m}")
+            q_run = q_lo[:, m, :].unsqueeze(2).to_broadcast([P, HALF_BLOCKS, RUN])
+            nc.vector.tensor_tensor(summed[:].rearrange("p (b r) -> p b r", r=RUN), p_acc[m][:].rearrange("p (b r) -> p b r", r=RUN), q_run, ALU.add)
+            return summed
+
+        def finish(pre, h, m):
+            res = keep.tile([P, BANK], F32, name=f"res{h}_{m}")
+            nc.vector.scalar_tensor_tensor(res[:], pre[:], 0.0, gate[:, h * BANK:(h + 1) * BANK], ALU.max, ALU.mult)
+            store(res, h, m)
+
+        summed = [add_context(0)]
+        for m in range(1, N // P):
+            summed.append(add_context(m))
+            finish(summed[m - 1], 0, m - 1)
+        finish(summed[-1], 0, N // P - 1)
+
+        for m in range(N // P):
+            acc = bank(4 + m)
+            cols = slice(m * P, (m + 1) * P)
+            pairs = acc[:].rearrange("p (b u e) -> p b u e", u=RUN // PAIR, e=PAIR)
+            for u in range(RUN // PAIR):
+                nc.tensor.matmul(pairs[:, :, u, :], lhsT=q_t[:, cols], rhs=ident[:], is_transpose=True, start=(u == 0), stop=False)
+            for i in range(BANK // P):
+                nc.tensor.matmul(acc[:, i * P:(i + 1) * P], lhsT=p_t[i][:, cols], rhs=ident[:], is_transpose=True,
+                                 start=False, stop=(i == BANK // P - 1))
+            finish(acc, 1, m)

@@ -21,17 +21,20 @@ P = 128
 PACK = 4
 RUN = 8
 BANK = 512
-HALVES = J // BANK
-HALF_BLOCKS = B // HALVES
+HALF_BLOCKS = BANK // RUN
+SLOT_TILES = BANK // P
+ROW_TILES = N // P
 LIST_COL = 16
+QUADRANT = 32
+SCALE_ROWS = 16
 PAIR = 2
 HEAD = 512
-PE_PLANES = 3
+TENSOR_SUMS = 3
 
 
 def load_scale_rows(nc, plane, scales):
     for r in range(4):
-        nc.sync.dma_start(out=plane[r:P:32, :].bitcast(I32), in_=scales[0, r:16:4, :].bitcast(I32))
+        nc.sync.dma_start(out=plane[r:P:QUADRANT, :].bitcast(I32), in_=scales[0, r:SCALE_ROWS:4, :].bitcast(I32))
 
 
 def tile_moe_expert_with_block_context_kernel(tc, xf, wc_words, wc_scales, xt_words, xt_scales, wa_words, wa_scales, ga, offs, out):
@@ -69,10 +72,10 @@ def tile_moe_expert_with_block_context_kernel(tc, xf, wc_words, wc_scales, xt_wo
         nc.sync.dma_start(out=xf_rows[1][:], in_=xf_by_slot[1])
         load_scale_rows(nc, wc_plane, wc_scales)
         nc.sync.dma_start(out=xf_rows[2][:], in_=xf_by_slot[2])
-        load_scale_rows(nc, wa_plane, wa_scales)
         nc.sync.dma_start(out=xf_rows[3][:], in_=xf_by_slot[3])
         nc.sync.dma_start(out=xt_codes[:], in_=xt_words[0].rearrange("p c r -> p (c r)").bitcast(I32))
         nc.sync.dma_start(out=wc_codes[:], in_=wc_words[0].rearrange("p c r -> p (c r)").bitcast(I32))
+        load_scale_rows(nc, wa_plane, wa_scales)
         nc.sync.dma_start(out=wa_codes[:].bitcast(I32), in_=wa_words[0].bitcast(I32))
 
         def half_list(h):
@@ -83,13 +86,13 @@ def tile_moe_expert_with_block_context_kernel(tc, xf, wc_words, wc_scales, xt_wo
         nc.tensor.transpose(turned[:, 0:P], ga_rows[:], ident[:])
         ga_cols = keep.tile([P, J // P], F32, name="ga_cols")
         nc.scalar.copy(ga_cols[:], turned[:, 0:J // P])
-        gate = keep.tile([P, J], F32, name="gate")
-        for h in range(HALVES):
-            spread = bank(6 + h)
-            for i in range(BANK // P):
-                s = h * (BANK // P) + i
-                nc.tensor.transpose(spread[:, i * P:(i + 1) * P], ga_cols[:, s:s + 1].to_broadcast([P, P]), ident[:])
-            nc.scalar.copy(gate[:, h * BANK:(h + 1) * BANK], spread[:])
+        spread = [bank(3), bank(7)]
+        for s in range(J // P):
+            h, i = divmod(s, SLOT_TILES)
+            nc.tensor.transpose(spread[h][:, i * P:(i + 1) * P], ga_cols[:, s:s + 1].to_broadcast([P, P]), ident[:])
+        gate_hi = keep.tile([P, BANK], F32, name="gate_hi")
+        nc.scalar.copy(gate_hi[:], spread[1][:])
+        gate = [spread[0], gate_hi]
 
         tok_plane = keep.tile([P, J], U8, name="tok_plane", align_bytes=64)
         nc.vector.tensor_copy(tok_plane[:], xt_plane[:].indirect(offsets[:]))
@@ -99,13 +102,13 @@ def tile_moe_expert_with_block_context_kernel(tc, xf, wc_words, wc_scales, xt_wo
             picked = keep.tile([P, J], F32, name=f"picked{t}", align_bytes=64)
             nc.vector.tensor_copy(picked[:], xf_rows[t][:].indirect(offsets[:]))
             runs = picked[:].rearrange("p (b r) -> p b r", r=RUN)
-            if t < PE_PLANES:
-                acc = bank(1 + t % 2)
+            if t < TENSOR_SUMS:
+                sums_acc = bank(1 + t % 2)
                 for r in range(RUN):
-                    nc.tensor.matmul(acc[:, 0:P], lhsT=runs[:, :, r], rhs=ident[:], is_transpose=True, start=(r == 0), stop=(r == RUN - 1))
+                    nc.tensor.matmul(sums_acc[:, 0:P], lhsT=runs[:, :, r], rhs=ident[:], is_transpose=True, start=(r == 0), stop=(r == RUN - 1))
                 sums_t = keep.tile([P, P], F32, name=f"sums_t{t}", align_bytes=64)
-                nc.scalar.copy(sums_t[:], acc[:, 0:P])
-                back = bank(3 + t % 2)
+                nc.scalar.copy(sums_t[:], sums_acc[:, 0:P])
+                back = bank(4 + t % 2)
                 nc.tensor.transpose(back[:, 0:P], sums_t[:], ident[:])
                 nc.scalar.copy(sums[:, t, :], back[:, 0:P])
             else:
@@ -129,66 +132,67 @@ def tile_moe_expert_with_block_context_kernel(tc, xf, wc_words, wc_scales, xt_wo
         tok_hi = keep.tile([P, BANK], U32, name="tok_hi", tag="staging", align_bytes=64)
         nc.vector.tensor_copy(tok_hi[:], xt_codes[:].bitcast(U32).indirect(half_list(1)))
 
-        q_acc = bank(0)
-        for m in range(N // P):
+        q_cols = ROW_TILES * HALF_BLOCKS
+        q_acc = bank(7)
+        for m in range(ROW_TILES):
             cols = slice(m * P, (m + 1) * P)
             nc.tensor.matmul_mx(out=q_acc[:, m * HALF_BLOCKS:(m + 1) * HALF_BLOCKS], lhsT=wc_codes[:, cols].bitcast(FP8X4), lhsT_scale=wc_plane[:, cols],
                                 rhs=lo_codes[:].bitcast(FP8X4), rhs_scale=lo_plane[:], start=True, stop=True)
-        q_lo = keep.tile([P, N // P, HALF_BLOCKS], F32, name="q_lo")
-        nc.scalar.copy(q_lo[:], q_acc[:, 0:N // P * HALF_BLOCKS].rearrange("p (m b) -> p m b", b=HALF_BLOCKS))
+        q_lo = keep.tile([P, q_cols, PAIR], F32, name="q_lo")
+        nc.scalar.copy(q_lo[:], q_acc[:, 0:q_cols].unsqueeze(2).to_broadcast([P, q_cols, PAIR]))
 
-        def store(res, h, m):
-            nc.sync.dma_start(out=out[m * P:(m + 1) * P, h * BANK:(h + 1) * BANK], in_=res[:])
-
-        def p_lo(m, b):
-            acc = bank(b)
-            nc.tensor.matmul_mx(out=acc[:], lhsT=wa_codes[:, 2 * m * P:2 * (m + 1) * P].bitcast(FP4X4), lhsT_scale=wa_plane[:, m * P:(m + 1) * P],
+        def p_lo(m, bank_index):
+            p_bank = bank(bank_index)
+            nc.tensor.matmul_mx(out=p_bank[:], lhsT=wa_codes[:, 2 * m * P:2 * (m + 1) * P].bitcast(FP4X4), lhsT_scale=wa_plane[:, m * P:(m + 1) * P],
                                 rhs=tok_lo[:].bitcast(FP8X4), rhs_scale=tok_plane[:, 0:BANK], start=True, stop=True)
-            return acc
+            return p_bank
 
-        p_acc = [p_lo(0, 2), p_lo(1, 3)]
+        p_acc = [p_lo(0, 0), p_lo(1, 1)]
 
-        qt_acc = bank(1)
+        qt_acc = bank(6)
         nc.tensor.matmul_mx(out=qt_acc[:], lhsT=hi_codes[:].bitcast(FP8X4), lhsT_scale=hi_plane[:],
                             rhs=wc_codes[:].bitcast(FP8X4), rhs_scale=wc_plane[:], start=True, stop=True)
         q_t = keep.tile([P, N], F32, name="q_t", align_bytes=64)
         nc.scalar.copy(q_t[:], qt_acc[:])
-        p_acc.extend([p_lo(2, 0), p_lo(3, 1)])
+        p_acc.append(p_lo(2, 2))
 
         p_t = []
-        for i in range(BANK // P):
-            acc = bank(4 + i)
-            nc.tensor.matmul_mx(out=acc[:], lhsT=tok_hi[:, i * P:(i + 1) * P].bitcast(FP8X4),
+        for i in range(SLOT_TILES):
+            pt_acc = bank(4 + i)
+            nc.tensor.matmul_mx(out=pt_acc[:], lhsT=tok_hi[:, i * P:(i + 1) * P].bitcast(FP8X4),
                                 lhsT_scale=tok_plane[:, BANK + i * P:BANK + (i + 1) * P],
                                 rhs=wa_codes[:].bitcast(FP4X4), rhs_scale=wa_plane[:], start=True, stop=True)
-            sb = keep.tile([P, N], F32, name=f"p_t{i}", align_bytes=64)
-            nc.scalar.copy(sb[:], acc[:])
-            p_t.append(sb)
+            pt_tile = keep.tile([P, N], F32, name=f"p_t{i}", align_bytes=64)
+            nc.scalar.copy(pt_tile[:], pt_acc[:])
+            p_t.append(pt_tile)
+
+        def in_pairs(tile):
+            return tile[:].rearrange("p (b u e) -> p b u e", u=RUN // PAIR, e=PAIR)
 
         def add_context(m):
-            summed = keep.tile([P, BANK], F32, name=f"summed{m}")
-            q_run = q_lo[:, m, :].unsqueeze(2).to_broadcast([P, HALF_BLOCKS, RUN])
-            nc.vector.tensor_tensor(summed[:].rearrange("p (b r) -> p b r", r=RUN), p_acc[m][:].rearrange("p (b r) -> p b r", r=RUN), q_run, ALU.add)
-            return summed
+            p_plus_q = keep.tile([P, BANK], F32, name=f"summed{m}")
+            q_run = q_lo[:, m * HALF_BLOCKS:(m + 1) * HALF_BLOCKS, :].unsqueeze(2).to_broadcast([P, HALF_BLOCKS, RUN // PAIR, PAIR])
+            nc.vector.tensor_tensor(in_pairs(p_plus_q), in_pairs(p_acc[m]), q_run, ALU.add)
+            return p_plus_q
 
-        def finish(pre, h, m):
+        def finish(p_plus_q, h, m):
             res = keep.tile([P, BANK], F32, name=f"res{h}_{m}")
-            nc.vector.scalar_tensor_tensor(res[:], pre[:], 0.0, gate[:, h * BANK:(h + 1) * BANK], ALU.max, ALU.mult)
-            store(res, h, m)
+            nc.vector.scalar_tensor_tensor(res[:], p_plus_q[:], 0.0, gate[h][:], ALU.max, ALU.mult)
+            nc.sync.dma_start(out=out[m * P:(m + 1) * P, h * BANK:(h + 1) * BANK], in_=res[:])
 
         summed = [add_context(0)]
-        for m in range(1, N // P):
+        p_acc.append(p_lo(3, 0))
+        for m in range(1, ROW_TILES):
             summed.append(add_context(m))
             finish(summed[m - 1], 0, m - 1)
-        finish(summed[-1], 0, N // P - 1)
+        finish(summed[-1], 0, ROW_TILES - 1)
 
-        for m in range(N // P):
-            acc = bank(4 + m)
+        for m in range(ROW_TILES):
+            sum_acc = bank(4 + m)
             cols = slice(m * P, (m + 1) * P)
-            pairs = acc[:].rearrange("p (b u e) -> p b u e", u=RUN // PAIR, e=PAIR)
             for u in range(RUN // PAIR):
-                nc.tensor.matmul(pairs[:, :, u, :], lhsT=q_t[:, cols], rhs=ident[:], is_transpose=True, start=(u == 0), stop=False)
-            for i in range(BANK // P):
-                nc.tensor.matmul(acc[:, i * P:(i + 1) * P], lhsT=p_t[i][:, cols], rhs=ident[:], is_transpose=True,
-                                 start=False, stop=(i == BANK // P - 1))
-            finish(acc, 1, m)
+                nc.tensor.matmul(in_pairs(sum_acc)[:, :, u, :], lhsT=q_t[:, cols], rhs=ident[:], is_transpose=True, start=(u == 0), stop=False)
+            for i in range(SLOT_TILES):
+                nc.tensor.matmul(sum_acc[:, i * P:(i + 1) * P], lhsT=p_t[i][:, cols], rhs=ident[:], is_transpose=True,
+                                 start=False, stop=(i == SLOT_TILES - 1))
+            finish(sum_acc, 1, m)

from contextlib import ExitStack

import concourse.mybir as mybir
from concourse.masks import make_identity

K, T, J, B, L, N = 512, 2048, 1024, 128, 512, 512
FLOPS = 2 * K * N * B + 2 * L * N * J

F32 = mybir.dt.float32
BF16 = mybir.dt.bfloat16
I32 = mybir.dt.int32
U32 = mybir.dt.uint32
U16 = mybir.dt.uint16
U8 = mybir.dt.uint8
FP8X4 = mybir.dt.float8_e4m3fn_x4
FP4X4 = mybir.dt.float4_e2m1fn_x4
ALU = mybir.AluOpType
ACT = mybir.ActivationFunctionType

P = 128
PACK = 4
RUN = 8
BANK = 512
HALF_BLOCKS = BANK // RUN
SLOT_TILES = BANK // P
ROW_TILES = N // P
LIST_COL = 16
QUADRANT = 32
SCALE_ROWS = 16
PAIR = 2
HEAD = 512
TENSOR_SUMS = 3


def load_scale_rows(nc, plane, scales):
    for r in range(4):
        nc.sync.dma_start(out=plane[r:P:QUADRANT, :].bitcast(I32), in_=scales[0, r:SCALE_ROWS:4, :].bitcast(I32))


def tile_moe_expert_with_block_context_kernel(tc, xf, wc_words, wc_scales, xt_words, xt_scales, wa_words, wa_scales, ga, offs, out):
    nc = tc.nc
    with ExitStack() as ctx:
        keep = ctx.enter_context(tc.tile_pool(name="keep", bufs=1))
        psum = ctx.enter_context(tc.psum_pool(name="psum", bufs=1))

        def bank(i):
            return psum.tile([P, BANK], F32, name=f"bank{i}", tag=f"bank{i}")

        offsets = keep.tile([P, J // LIST_COL], U16, name="offsets")
        xt_plane = keep.tile([P, T], U8, name="xt_plane", align_bytes=64)
        wa_plane = keep.tile([P, N], U8, name="wa_plane", align_bytes=64)
        wc_plane = keep.tile([P, N], U8, name="wc_plane", align_bytes=64)
        xt_codes = keep.tile([P, T], I32, name="xt_codes", align_bytes=64)
        wa_codes = keep.tile([P, 2 * N], U8, name="wa_codes", align_bytes=64)
        wc_codes = keep.tile([P, N], I32, name="wc_codes", align_bytes=64)
        xf_rows = [keep.tile([P, T], F32, name=f"xf_rows{t}", align_bytes=64) for t in range(PACK)]
        ga_rows = keep.tile([P, P], F32, name="ga_rows", align_bytes=64)
        ident = keep.tile([P, P], F32, name="ident", align_bytes=64)

        nc.vector.memset(xt_plane[:].bitcast(I32), 0)
        nc.vector.memset(ga_rows[:], 0.0)
        nc.vector.memset(wa_plane[:].bitcast(I32), 0)
        nc.vector.memset(wc_plane[:].bitcast(I32), 0)
        make_identity(nc, ident[:])

        xf_by_slot = xf.rearrange("(p t) c -> t p c", t=PACK)
        nc.sync.dma_start(offsets[:], offs)
        nc.sync.dma_start(out=xf_rows[0][:, 0:HEAD], in_=xf_by_slot[0][:, 0:HEAD])
        load_scale_rows(nc, xt_plane, xt_scales)
        nc.sync.dma_start(out=xf_rows[0][:, HEAD:T], in_=xf_by_slot[0][:, HEAD:T])
        nc.sync.dma_start(out=ga_rows[0:J // P, :], in_=ga.rearrange("o (s i) -> (o s) i", i=P))
        nc.sync.dma_start(out=xf_rows[1][:], in_=xf_by_slot[1])
        load_scale_rows(nc, wc_plane, wc_scales)
        nc.sync.dma_start(out=xf_rows[2][:], in_=xf_by_slot[2])
        nc.sync.dma_start(out=xf_rows[3][:], in_=xf_by_slot[3])
        nc.sync.dma_start(out=xt_codes[:], in_=xt_words[0].rearrange("p c r -> p (c r)").bitcast(I32))
        nc.sync.dma_start(out=wc_codes[:], in_=wc_words[0].rearrange("p c r -> p (c r)").bitcast(I32))
        load_scale_rows(nc, wa_plane, wa_scales)
        nc.sync.dma_start(out=wa_codes[:].bitcast(I32), in_=wa_words[0].bitcast(I32))

        def half_list(h):
            cols = BANK // LIST_COL
            return offsets[:, h * cols:(h + 1) * cols]

        turned = bank(0)
        nc.tensor.transpose(turned[:, 0:P], ga_rows[:], ident[:])
        ga_cols = keep.tile([P, J // P], F32, name="ga_cols")
        nc.scalar.copy(ga_cols[:], turned[:, 0:J // P])
        spread = [bank(3), bank(7)]
        for s in range(J // P):
            h, i = divmod(s, SLOT_TILES)
            nc.tensor.transpose(spread[h][:, i * P:(i + 1) * P], ga_cols[:, s:s + 1].to_broadcast([P, P]), ident[:])
        gate_hi = keep.tile([P, BANK], F32, name="gate_hi")
        nc.scalar.copy(gate_hi[:], spread[1][:])
        gate = [spread[0], gate_hi]

        tok_plane = keep.tile([P, J], U8, name="tok_plane", align_bytes=64)
        nc.vector.tensor_copy(tok_plane[:], xt_plane[:].indirect(offsets[:]))

        sums = keep.tile([P, PACK, B], F32, name="sums")
        for t in range(PACK):
            picked = keep.tile([P, J], F32, name=f"picked{t}", align_bytes=64)
            nc.vector.tensor_copy(picked[:], xf_rows[t][:].indirect(offsets[:]))
            runs = picked[:].rearrange("p (b r) -> p b r", r=RUN)
            if t < TENSOR_SUMS:
                sums_acc = bank(1 + t % 2)
                for r in range(RUN):
                    nc.tensor.matmul(sums_acc[:, 0:P], lhsT=runs[:, :, r], rhs=ident[:], is_transpose=True, start=(r == 0), stop=(r == RUN - 1))
                sums_t = keep.tile([P, P], F32, name=f"sums_t{t}", align_bytes=64)
                nc.scalar.copy(sums_t[:], sums_acc[:, 0:P])
                back = bank(4 + t % 2)
                nc.tensor.transpose(back[:, 0:P], sums_t[:], ident[:])
                nc.scalar.copy(sums[:, t, :], back[:, 0:P])
            else:
                nc.vector.tensor_reduce(sums[:, t, :], runs, mybir.AxisListType.X, ALU.add)

        by_block = sums[:].rearrange("p t b -> p b t")
        m2_lo = keep.tile([P, HALF_BLOCKS, PACK], BF16, name="m2_lo", align_bytes=64)
        nc.scalar.activation(m2_lo[:], by_block[:, 0:HALF_BLOCKS, :], ACT.Copy, scale=2.0 / RUN)
        m2_hi = keep.tile([P, HALF_BLOCKS, PAIR, PACK], BF16, name="m2_hi", tag="staging", align_bytes=64)
        twice = by_block[:, HALF_BLOCKS:B, :].unsqueeze(2).to_broadcast([P, HALF_BLOCKS, PAIR, PACK])
        nc.scalar.activation(m2_hi[:], twice, ACT.Copy, scale=2.0 / RUN)

        tok_lo = keep.tile([P, BANK], U32, name="tok_lo", align_bytes=64)
        nc.vector.tensor_copy(tok_lo[:], xt_codes[:].bitcast(U32).indirect(half_list(0)))
        lo_codes = keep.tile([P, HALF_BLOCKS], U32, name="lo_codes", align_bytes=64)
        lo_plane = keep.tile([P, HALF_BLOCKS], U8, name="lo_plane", align_bytes=64)
        nc.vector.quantize_mx(out=lo_codes[:].bitcast(FP8X4), scales=lo_plane[:], in_=m2_lo[:].rearrange("p b t -> p (b t)"))
        hi_codes = keep.tile([P, P], U32, name="hi_codes", align_bytes=64)
        hi_plane = keep.tile([P, P], U8, name="hi_plane", align_bytes=64)
        nc.vector.quantize_mx(out=hi_codes[:].bitcast(FP8X4), scales=hi_plane[:], in_=m2_hi[:].rearrange("p b d t -> p (b d t)"))
        tok_hi = keep.tile([P, BANK], U32, name="tok_hi", tag="staging", align_bytes=64)
        nc.vector.tensor_copy(tok_hi[:], xt_codes[:].bitcast(U32).indirect(half_list(1)))

        q_cols = ROW_TILES * HALF_BLOCKS
        q_acc = bank(7)
        for m in range(ROW_TILES):
            cols = slice(m * P, (m + 1) * P)
            nc.tensor.matmul_mx(out=q_acc[:, m * HALF_BLOCKS:(m + 1) * HALF_BLOCKS], lhsT=wc_codes[:, cols].bitcast(FP8X4), lhsT_scale=wc_plane[:, cols],
                                rhs=lo_codes[:].bitcast(FP8X4), rhs_scale=lo_plane[:], start=True, stop=True)
        q_lo = keep.tile([P, q_cols, PAIR], F32, name="q_lo")
        nc.scalar.copy(q_lo[:], q_acc[:, 0:q_cols].unsqueeze(2).to_broadcast([P, q_cols, PAIR]))

        def p_lo(m, bank_index):
            p_bank = bank(bank_index)
            nc.tensor.matmul_mx(out=p_bank[:], lhsT=wa_codes[:, 2 * m * P:2 * (m + 1) * P].bitcast(FP4X4), lhsT_scale=wa_plane[:, m * P:(m + 1) * P],
                                rhs=tok_lo[:].bitcast(FP8X4), rhs_scale=tok_plane[:, 0:BANK], start=True, stop=True)
            return p_bank

        p_acc = [p_lo(0, 0), p_lo(1, 1)]

        qt_acc = bank(6)
        nc.tensor.matmul_mx(out=qt_acc[:], lhsT=hi_codes[:].bitcast(FP8X4), lhsT_scale=hi_plane[:],
                            rhs=wc_codes[:].bitcast(FP8X4), rhs_scale=wc_plane[:], start=True, stop=True)
        q_t = keep.tile([P, N], F32, name="q_t", align_bytes=64)
        nc.scalar.copy(q_t[:], qt_acc[:])
        p_acc.append(p_lo(2, 2))

        p_t = []
        for i in range(SLOT_TILES):
            pt_acc = bank(4 + i)
            nc.tensor.matmul_mx(out=pt_acc[:], lhsT=tok_hi[:, i * P:(i + 1) * P].bitcast(FP8X4),
                                lhsT_scale=tok_plane[:, BANK + i * P:BANK + (i + 1) * P],
                                rhs=wa_codes[:].bitcast(FP4X4), rhs_scale=wa_plane[:], start=True, stop=True)
            pt_tile = keep.tile([P, N], F32, name=f"p_t{i}", align_bytes=64)
            nc.scalar.copy(pt_tile[:], pt_acc[:])
            p_t.append(pt_tile)

        def in_pairs(tile):
            return tile[:].rearrange("p (b u e) -> p b u e", u=RUN // PAIR, e=PAIR)

        def add_context(m):
            p_plus_q = keep.tile([P, BANK], F32, name=f"summed{m}")
            q_run = q_lo[:, m * HALF_BLOCKS:(m + 1) * HALF_BLOCKS, :].unsqueeze(2).to_broadcast([P, HALF_BLOCKS, RUN // PAIR, PAIR])
            nc.vector.tensor_tensor(in_pairs(p_plus_q), in_pairs(p_acc[m]), q_run, ALU.add)
            return p_plus_q

        def finish(p_plus_q, h, m):
            res = keep.tile([P, BANK], F32, name=f"res{h}_{m}")
            nc.vector.scalar_tensor_tensor(res[:], p_plus_q[:], 0.0, gate[h][:], ALU.max, ALU.mult)
            nc.sync.dma_start(out=out[m * P:(m + 1) * P, h * BANK:(h + 1) * BANK], in_=res[:])

        summed = [add_context(0)]
        p_acc.append(p_lo(3, 0))
        for m in range(1, ROW_TILES):
            summed.append(add_context(m))
            finish(summed[m - 1], 0, m - 1)
        finish(summed[-1], 0, ROW_TILES - 1)

        for m in range(ROW_TILES):
            sum_acc = bank(4 + m)
            cols = slice(m * P, (m + 1) * P)
            for u in range(RUN // PAIR):
                nc.tensor.matmul(in_pairs(sum_acc)[:, :, u, :], lhsT=q_t[:, cols], rhs=ident[:], is_transpose=True, start=(u == 0), stop=False)
            for i in range(SLOT_TILES):
                nc.tensor.matmul(sum_acc[:, i * P:(i + 1) * P], lhsT=p_t[i][:, cols], rhs=ident[:], is_transpose=True,
                                 start=False, stop=(i == SLOT_TILES - 1))
            finish(sum_acc, 1, m)
